import numpy as np
import ml_dtypes


def mxq(x, axis, fmt="e4m3"):
    dtype, down = {"e4m3": (ml_dtypes.float8_e4m3fn, 7), "e5m2": (ml_dtypes.float8_e5m2, 14)}[fmt]
    v = np.moveaxis(np.asarray(x, np.float32).astype(ml_dtypes.bfloat16).astype(np.float64), axis, -1)
    blocks = v.reshape(v.shape[:-1] + (-1, 32))
    amax = np.abs(blocks).max(-1, keepdims=True)
    byte = np.maximum(np.where(amax > 0, np.frexp(amax)[1] - 1 + 127, 0) - down, 1)
    scale = np.exp2(byte - 127.0)
    codes = (blocks / scale).astype(np.float32).astype(dtype).astype(np.float64)
    return np.moveaxis((codes * scale).reshape(v.shape), -1, axis)


WIDE = False


def mx_kscale(k):
    if not WIDE:
        return np.ones(k)
    levels = np.array([10, -10, 5, -5, 0])
    if k % 512:
        return np.exp2(np.random.permutation(np.resize(levels, k // 32))).repeat(32)
    a = np.empty((k // 512, 16))
    for p in range(k // 512):
        a[p, :8] = np.random.permutation(np.resize(levels, 8))
        for g in range(8):
            far = levels[np.abs(levels - a[p, g]) >= 10]
            a[p, g + 8] = far[np.random.randint(len(far))]
    return np.exp2(a.ravel()).repeat(32)


def f64(x):
    return np.asarray(x).astype(np.float64)


def striped(idx):
    return np.tile(idx.reshape(-1, 16).T, (8, 1)).astype(np.uint16)


def unstriped(offs):
    return offs[:16].T.reshape(-1).astype(np.int64)


def pack_weight(w):
    k, n = w.shape
    w = f64(np.asarray(w, np.float32).astype(ml_dtypes.bfloat16)).reshape(k // 32, 32, n)
    amax = np.abs(w).max(1)
    byte = np.clip(np.where(amax > 0, np.frexp(amax)[1] - 1 + 127 - 7, 1), 1, 254)
    scaled = (w * np.exp2(127.0 - byte)[:, None, :]).reshape(k, n).astype(np.float32)
    words = np.ascontiguousarray(scaled.reshape(k // 512, 128, 4, n).transpose(0, 1, 3, 2)).astype(ml_dtypes.float8_e4m3fn).view(np.uint8)
    return words, np.ascontiguousarray(byte.astype(np.uint8).reshape(k // 512, 16, n))


def unpack_weight(words, scales):
    g, p, n, _ = words.shape
    vals = np.ascontiguousarray(words).view(ml_dtypes.float8_e4m3fn).astype(np.float64) * np.repeat(np.exp2(scales.astype(np.float64) - 127.0), 8, axis=1)[..., None]
    return vals.transpose(0, 1, 3, 2).reshape(g * 512, n)


def sigmoid(v):
    return 1.0 / (1.0 + np.exp(-np.maximum(v, -700.0)))


K, T, S, V, D = 512, 1024, 512, 512, 2
P = 2 ** 7


def setup_inputs():
    n = np.random.standard_normal
    s = mx_kscale(K)[:, None]
    packed_xT = pack_weight(n((K, T)) * s)
    return {
        "x_words": packed_xT[0],
        "x_scales": packed_xT[1],
        "hT": (n((K, V)) / np.sqrt(K) / s).astype(np.float32),
        "delta": (np.tile(n((D, 1, S)), (1, P, 1))).astype(np.float32),
        "offs": striped(np.random.permutation(T)[:S]),
        "pos1": striped(np.random.permutation(S)),
        "pos2": striped(np.random.permutation(S)),
    }


def reference(x_words, x_scales, hT, delta, offs, pos1, pos2):
    hTq = mxq(f64(hT), 0, "e4m3")
    xq = unpack_weight(x_words, x_scales)[:, unstriped(offs)]
    y = hTq.T @ xq
    return (sigmoid(y[:, unstriped(pos1)] - y)) * f64(delta)[0, :1] + (sigmoid(y[:, unstriped(pos2)] - y)) * f64(delta)[1, :1]

@@ -1,0 +1,206 @@
+from contextlib import ExitStack
+
+import concourse.mybir as mybir
+from concourse.masks import make_identity
+
+K, T, S, V, D = 512, 1024, 512, 512, 2
+P = 128
+PACK = 4
+BLOCKS = V // P
+CHUNKS = S // P
+WINDOW = 2048
+FLOPS = 2 * K * V * S
+
+F32 = mybir.dt.float32
+BF16 = mybir.dt.bfloat16
+I32 = mybir.dt.int32
+U32 = mybir.dt.uint32
+U16 = mybir.dt.uint16
+U8 = mybir.dt.uint8
+FP8X4 = mybir.dt.float8_e4m3fn_x4
+MULT = mybir.AluOpType.mult
+ADD = mybir.AluOpType.add
+SIGMOID = mybir.ActivationFunctionType.Sigmoid
+COPY = mybir.ActivationFunctionType.Copy
+
+
+def tile_picked_yndcg_lam_p_kernel(tc, x_words, x_scales, hT, delta, offs, pos1, pos2, out):
+    nc = tc.nc
+    with ExitStack() as ctx:
+        keep = ctx.enter_context(tc.tile_pool(name="keep", bufs=1))
+        psum = ctx.enter_context(tc.psum_pool(name="psum", bufs=1))
+
+        picks = keep.tile([P, S // 16], U16, name="picks")
+        rivals = [keep.tile([P, S // 16], U16, name="rivals%d" % d) for d in range(D)]
+        words = keep.tile([P, T], U32, name="words", align_bytes=64)
+        scales = keep.tile([P, T], U8, name="scales", align_bytes=64)
+        h_first = keep.tile([P, P, PACK], BF16, name="h_first", tag="x_codes", align_bytes=64)
+        x_plane = keep.tile([P, S], U8, name="x_plane", align_bytes=64)
+        ident = keep.tile([P, P], F32, name="ident")
+        warm = keep.tile([P, 8], F32, name="warm")
+        delta_rows = keep.tile([P, P], F32, name="delta_rows")
+        delta_cols = keep.tile([P, D * CHUNKS], F32, name="delta_cols")
+
+        nc.vector.memset(scales[:].bitcast(I32), 0)
+        nc.vector.memset(warm[:], 0.0)
+        h_rows = hT.rearrange("(p j) t -> p j t", j=PACK)
+        h_raw = [keep.tile([P, PACK, P], F32, name="h_raw%d" % b) for b in range(BLOCKS)]
+        nc.scalar.dma_start(h_raw[0][:], h_rows[:, :, 0:P])
+        nc.sync.dma_start(picks[:], offs)
+        for q in range(4):
+            (nc.sync, nc.scalar)[q % 2].dma_start(scales[32 * q : 32 * q + 4, :].bitcast(I32), x_scales[0, 4 * q : 4 * q + 4, :].bitcast(I32))
+        nc.scalar.activation(warm[:, 0:1], warm[:, 1:2], SIGMOID)
+        nc.sync.dma_start(words[:].bitcast(I32), x_words[0].rearrange("p n t -> p (n t)").bitcast(I32))
+        nc.sync.dma_start(h_raw[1][:], h_rows[:, :, P : 2 * P])
+        nc.sync.dma_start(rivals[0][:], pos1)
+        make_identity(nc, ident[:])
+        nc.gpsimd.memset(delta_rows[:], 0.0)
+        for d in range(D):
+            nc.sync.dma_start(delta_rows[d * CHUNKS : (d + 1) * CHUNKS, :], delta[d, 0, :].rearrange("(c m) -> c m", m=P))
+        nc.sync.dma_start(rivals[1][:], pos2)
+        for b in range(2, BLOCKS):
+            nc.sync.dma_start(h_raw[b][:], h_rows[:, :, b * P : (b + 1) * P])
+
+        h_bf = keep.tile([P, P, PACK], BF16, name="h_bf", align_bytes=64)
+        h_codes = keep.tile([P, P], U32, name="h_codes", align_bytes=64)
+        h_plane = keep.tile([P, P], U8, name="h_plane", align_bytes=64)
+        last = BLOCKS - 1
+        scores = [keep.tile([P, WINDOW], F32, name="scores%d" % b) for b in range(last)]
+        scores.append(keep.tile([P, S], F32, name="scores_last"))
+        negated = keep.tile([P, S], F32, name="negated")
+
+        def cast(b, h_bf):
+            nc.scalar.copy(
+                h_bf[:].rearrange("p (c i) j -> p c j i", i=4),
+                h_raw[b][:].rearrange("p j (c i) -> p c j i", i=4),
+            )
+
+        def quantize(h_bf):
+            nc.vector.quantize_mx(out=h_codes[:].bitcast(FP8X4), scales=h_plane[:], in_=h_bf[:].rearrange("p t j -> p (t j)"))
+
+        def product(b, lo, hi, tag="y_bank"):
+            bank = psum.tile([P, hi - lo], F32, name=tag, bufs=2)
+            nc.tensor.matmul_mx(
+                out=bank[:],
+                lhsT=h_codes[:].bitcast(FP8X4),
+                lhsT_scale=h_plane[:],
+                rhs=x_codes[:, lo:hi].bitcast(FP8X4),
+                rhs_scale=x_plane[:, lo:hi],
+                start=True,
+                stop=True,
+            )
+            if tag == "y_bank":
+                nc.scalar.copy(scores[b][:, lo:hi], bank[:])
+            else:
+                nc.vector.tensor_copy(scores[b][:, lo:hi], bank[:])
+            if b == last:
+                nc.scalar.activation(negated[:], bank[:], COPY, scale=-1.0)
+
+        half = S // 2
+        nc.vector.tensor_copy(x_plane[:], scales[:].indirect(picks[:]))
+        cast(0, h_first)
+        quantize(h_first)
+        cast(1, h_bf)
+        x_codes = keep.tile([P, S], U32, name="x_codes", tag="x_codes", align_bytes=64)
+        for lo, hi, tag in ((0, half, "y_bank"), (half, half + P, "y_bank"), (half + P, S, "out_bank")):
+            nc.vector.tensor_copy(x_codes[:, lo:hi], words[:].indirect(picks[:, lo // 16 : hi // 16]))
+            product(0, lo, hi, tag)
+
+        turned = psum.tile([P, P], F32, name="y_bank", bufs=2)
+        nc.tensor.transpose(turned[:], delta_rows[:], ident[:])
+        nc.scalar.copy(delta_cols[:], turned[:, 0 : D * CHUNKS])
+
+        units = [(b, [(d, c) for c in range(CHUNKS)]) for b in range(last) for d in range(D)]
+        whole = len(units)
+        for chunks in ((0, 1), (2,), (3,)):
+            units.append((last, [(d, c) for d in range(D) for c in chunks]))
+        odds = [keep.tile([P, len(un[1]) * P], F32, name="odds%d" % u) for u, un in enumerate(units)]
+        terms = [keep.tile([P, len(un[1]) * P], F32, name="terms%d" % u) for u, un in enumerate(units)]
+        fresh = [keep.tile([P, S], F32, name="fresh%d" % u) for u in range(4)]
+        diff = {}
+
+        def at(i):
+            return slice(i * P, (i + 1) * P)
+
+        def seed(u):
+            b, parts = units[u]
+            bank = psum.tile([P, len(parts) * P], F32, name="diff_bank", bufs=4)
+            diff[u] = bank
+            own = negated if b == last else scores[b]
+            for i, (d, c) in enumerate(parts):
+                nc.tensor.matmul(bank[:, at(i)], own[:, at(c)], ident[:], start=(i == 0), stop=False, is_transpose=True)
+
+        def turn(u, src, first, count):
+            n = len(units[u][1])
+            for i in range(count):
+                nc.tensor.matmul(diff[u][:, at(first + i)], src[:, at(i)], ident[:], start=False, stop=(first + i == n - 1), is_transpose=True)
+
+        def squash(u):
+            nc.scalar.activation(odds[u][:], diff[u][:], SIGMOID, scale=(1.0 if units[u][0] == last else -1.0))
+
+        def weigh(u):
+            for i, (d, c) in enumerate(units[u][1]):
+                k = d * CHUNKS + c
+                nc.vector.tensor_scalar(terms[u][:, at(i)], odds[u][:, at(i)], delta_cols[:, k : k + 1], None, MULT)
+
+        def finish(b, chunks, source, tag):
+            bank = psum.tile([P, len(chunks) * P], F32, name=tag, bufs=2)
+            for i, c in enumerate(chunks):
+                for d in range(D):
+                    nc.tensor.matmul(bank[:, at(i)], source(d, i), ident[:], start=(d == 0), stop=(d == D - 1), is_transpose=True)
+            result = keep.tile([P, len(chunks) * P], F32, name="result%d_%d" % (b, chunks[0]))
+            nc.scalar.copy(result[:], bank[:])
+            nc.sync.dma_start(out[at(b), chunks[0] * P : (chunks[-1] + 1) * P], result[:])
+
+        def weigh_whole(u):
+            weigh(u)
+            if u % D == D - 1:
+                finish(u // D, tuple(range(CHUNKS)), lambda d, i: terms[u - 1 + d][:, at(i)], "out_bank")
+
+        LAG = 4
+        for u in range(whole):
+            b, d = u // D, u % D
+            if u >= LAG:
+                weigh_whole(u - LAG)
+            if d == 0:
+                quantize(h_bf)
+                if b + 2 < BLOCKS:
+                    cast(b + 2, h_bf)
+                seed(u)
+                seed(u + 1)
+                product(b + 1, 0, S)
+            dst = fresh[u] if u < LAG else odds[u - LAG]
+            nc.vector.tensor_scalar(dst[:], scores[b][:].indirect(rivals[d][:]), -1.0, 0.0, MULT, ADD)
+            turn(u, dst, 0, CHUNKS)
+            squash(u)
+
+        def small(u, d, dst):
+            parts = units[u][1]
+            n = len(parts) // D
+            c0 = parts[0][1]
+            nc.vector.tensor_copy(dst, scores[last][:].indirect(rivals[d][:, c0 * 8 : (c0 + n) * 8]))
+            turn(u, dst, d * n, n)
+
+        ua, ub, uc = whole, whole + 1, whole + 2
+        weigh_whole(2)
+        seed(ua)
+        small(ua, 0, odds[2][:, 0:half])
+        weigh_whole(3)
+        small(ua, 1, odds[3][:, 0:half])
+        squash(ua)
+        weigh_whole(4)
+        seed(ub)
+        small(ub, 0, odds[4][:, 0:P])
+        small(ub, 1, odds[4][:, P : 2 * P])
+        squash(ub)
+        weigh_whole(5)
+        seed(uc)
+        small(uc, 0, odds[5][:, 0:P])
+        small(uc, 1, odds[5][:, P : 2 * P])
+        squash(uc)
+        weigh(ua)
+        finish(last, (0, 1), lambda d, i: terms[ua][:, at(2 * d + i)], "y_bank")
+        weigh(ub)
+        finish(last, (2,), lambda d, i: terms[ub][:, at(d)], "y_bank")
+        weigh(uc)
+        finish(last, (3,), lambda d, i: terms[uc][:, at(d)], "out_bank")

@@ -32,7 +32,7 @@ def tile_picked_yndcg_lam_p_kernel(tc, x_words, x_scales, hT, delta, offs, pos1,
 
         picks = keep.tile([P, S // 16], U16, name="picks")
         rivals = [keep.tile([P, S // 16], U16, name="rivals%d" % d) for d in range(D)]
-        words = keep.tile([P, T], U32, name="words", align_bytes=64)
+        words = keep.tile([P, T], U32, name="words", tag="words", align_bytes=64)
         scales = keep.tile([P, T], U8, name="scales", align_bytes=64)
         h_first = keep.tile([P, P, PACK], BF16, name="h_first", tag="x_codes", align_bytes=64)
         x_plane = keep.tile([P, S], U8, name="x_plane", align_bytes=64)
@@ -51,64 +51,75 @@ def tile_picked_yndcg_lam_p_kernel(tc, x_words, x_scales, hT, delta, offs, pos1,
             (nc.sync, nc.scalar)[q % 2].dma_start(scales[32 * q : 32 * q + 4, :].bitcast(I32), x_scales[0, 4 * q : 4 * q + 4, :].bitcast(I32))
         nc.scalar.activation(warm[:, 0:1], warm[:, 1:2], SIGMOID)
         nc.sync.dma_start(words[:].bitcast(I32), x_words[0].rearrange("p n t -> p (n t)").bitcast(I32))
-        nc.sync.dma_start(h_raw[1][:], h_rows[:, :, P : 2 * P])
+        for b in range(1, BLOCKS):
+            nc.sync.dma_start(h_raw[b][:], h_rows[:, :, b * P : (b + 1) * P])
         nc.sync.dma_start(rivals[0][:], pos1)
+        nc.sync.dma_start(rivals[1][:], pos2)
         make_identity(nc, ident[:])
         nc.gpsimd.memset(delta_rows[:], 0.0)
         for d in range(D):
             nc.sync.dma_start(delta_rows[d * CHUNKS : (d + 1) * CHUNKS, :], delta[d, 0, :].rearrange("(c m) -> c m", m=P))
-        nc.sync.dma_start(rivals[1][:], pos2)
-        for b in range(2, BLOCKS):
-            nc.sync.dma_start(h_raw[b][:], h_rows[:, :, b * P : (b + 1) * P])
 
-        h_bf = keep.tile([P, P, PACK], BF16, name="h_bf", align_bytes=64)
-        h_codes = keep.tile([P, P], U32, name="h_codes", align_bytes=64)
-        h_plane = keep.tile([P, P], U8, name="h_plane", align_bytes=64)
+        h_bf = [h_first] + [keep.tile([P, P, PACK], BF16, name="h_bf%d" % b, align_bytes=64) for b in (1, 2)]
+        h_codes = [keep.tile([P, P], U32, name="h_codes0", tag="relay", align_bytes=64)[:]]
+        h_plane = [keep.tile([P, P], U8, name="h_plane%d" % b, align_bytes=64) for b in range(BLOCKS)]
         last = BLOCKS - 1
         scores = [keep.tile([P, WINDOW], F32, name="scores%d" % b) for b in range(last)]
         scores.append(keep.tile([P, S], F32, name="scores_last"))
         negated = keep.tile([P, S], F32, name="negated")
 
-        def cast(b, h_bf):
+        def cast(b):
             nc.scalar.copy(
-                h_bf[:].rearrange("p (c i) j -> p c j i", i=4),
+                h_bf[b][:].rearrange("p (c i) j -> p c j i", i=4),
                 h_raw[b][:].rearrange("p j (c i) -> p c j i", i=4),
             )
 
-        def quantize(h_bf):
-            nc.vector.quantize_mx(out=h_codes[:].bitcast(FP8X4), scales=h_plane[:], in_=h_bf[:].rearrange("p t j -> p (t j)"))
+        def quantize(b):
+            nc.vector.quantize_mx(out=h_codes[b].bitcast(FP8X4), scales=h_plane[b][:], in_=h_bf[b][:].rearrange("p t j -> p (t j)"))
 
-        def product(b, lo, hi, tag="y_bank"):
+        def product(b, lo, hi, tag):
             bank = psum.tile([P, hi - lo], F32, name=tag, bufs=2)
             nc.tensor.matmul_mx(
                 out=bank[:],
-                lhsT=h_codes[:].bitcast(FP8X4),
-                lhsT_scale=h_plane[:],
+                lhsT=h_codes[b].bitcast(FP8X4),
+                lhsT_scale=h_plane[b][:],
                 rhs=x_codes[:, lo:hi].bitcast(FP8X4),
                 rhs_scale=x_plane[:, lo:hi],
                 start=True,
                 stop=True,
             )
-            if tag == "y_bank":
-                nc.scalar.copy(scores[b][:, lo:hi], bank[:])
-            else:
+            if b == 0 and hi == S:
                 nc.vector.tensor_copy(scores[b][:, lo:hi], bank[:])
+            else:
+                nc.scalar.copy(scores[b][:, lo:hi], bank[:])
             if b == last:
                 nc.scalar.activation(negated[:], bank[:], COPY, scale=-1.0)
 
         half = S // 2
         nc.vector.tensor_copy(x_plane[:], scales[:].indirect(picks[:]))
-        cast(0, h_first)
-        quantize(h_first)
-        cast(1, h_bf)
+        cast(0)
+        quantize(0)
+        cast(1)
+        cast(2)
         x_codes = keep.tile([P, S], U32, name="x_codes", tag="x_codes", align_bytes=64)
         for lo, hi, tag in ((0, half, "y_bank"), (half, half + P, "y_bank"), (half + P, S, "out_bank")):
             nc.vector.tensor_copy(x_codes[:, lo:hi], words[:].indirect(picks[:, lo // 16 : hi // 16]))
             product(0, lo, hi, tag)
+        h_later = keep.tile([P, last, P], U32, name="h_later", tag="words", align_bytes=64)
+        h_codes.extend(h_later[:, b, :] for b in range(last))
+        h_bf.append(keep.tile([P, P, PACK], BF16, name="h_bf3", tag="relay", align_bytes=64))
+        cast(3)
+        quantize(1)
+        product(1, 0, S, "out_bank")
+        quantize(2)
+        product(2, 0, S, "y_bank")
 
         turned = psum.tile([P, P], F32, name="y_bank", bufs=2)
         nc.tensor.transpose(turned[:], delta_rows[:], ident[:])
         nc.scalar.copy(delta_cols[:], turned[:, 0 : D * CHUNKS])
+
+        quantize(3)
+        product(3, 0, S, "y_bank")
 
         units = [(b, [(d, c) for c in range(CHUNKS)]) for b in range(last) for d in range(D)]
         whole = len(units)
@@ -116,7 +127,9 @@ def tile_picked_yndcg_lam_p_kernel(tc, x_words, x_scales, hT, delta, offs, pos1,
             units.append((last, [(d, c) for d in range(D) for c in chunks]))
         odds = [keep.tile([P, len(un[1]) * P], F32, name="odds%d" % u) for u, un in enumerate(units)]
         terms = [keep.tile([P, len(un[1]) * P], F32, name="terms%d" % u) for u, un in enumerate(units)]
-        fresh = [keep.tile([P, S], F32, name="fresh%d" % u) for u in range(4)]
+        first = keep.tile([P, S], F32, name="first")
+        early = keep.tile([P, 3 * S], F32, name="early", tag="relay", align_bytes=64)
+        fresh = [first[:]] + [early[:, n * S : (n + 1) * S] for n in range(3)]
         diff = {}
 
         def at(i):
@@ -138,24 +151,36 @@ def tile_picked_yndcg_lam_p_kernel(tc, x_words, x_scales, hT, delta, offs, pos1,
         def squash(u):
             nc.scalar.activation(odds[u][:], diff[u][:], SIGMOID, scale=(1.0 if units[u][0] == last else -1.0))
 
-        def weigh(u):
-            for i, (d, c) in enumerate(units[u][1]):
-                k = d * CHUNKS + c
-                nc.vector.tensor_scalar(terms[u][:, at(i)], odds[u][:, at(i)], delta_cols[:, k : k + 1], None, MULT)
+        def factor(d, c):
+            k = d * CHUNKS + c
+            return delta_cols[:, k : k + 1]
 
-        def finish(b, chunks, source, tag):
+        def scale_on_vector(dst, src, d, c):
+            nc.vector.tensor_scalar(dst, src, factor(d, c), None, MULT)
+
+        def scale_and_add(dst, src, d, c, other):
+            nc.vector.scalar_tensor_tensor(dst, src, factor(d, c), other, MULT, ADD)
+
+        def finish(b, chunks, sources, tag):
             bank = psum.tile([P, len(chunks) * P], F32, name=tag, bufs=2)
-            for i, c in enumerate(chunks):
-                for d in range(D):
-                    nc.tensor.matmul(bank[:, at(i)], source(d, i), ident[:], start=(d == 0), stop=(d == D - 1), is_transpose=True)
+            for i in range(len(chunks)):
+                parts = sources(i)
+                for n, part in enumerate(parts):
+                    nc.tensor.matmul(bank[:, at(i)], part, ident[:], start=(n == 0), stop=(n == len(parts) - 1), is_transpose=True)
             result = keep.tile([P, len(chunks) * P], F32, name="result%d_%d" % (b, chunks[0]))
             nc.scalar.copy(result[:], bank[:])
             nc.sync.dma_start(out[at(b), chunks[0] * P : (chunks[-1] + 1) * P], result[:])
 
+        ON_SCALAR = 2
+
         def weigh_whole(u):
-            weigh(u)
-            if u % D == D - 1:
-                finish(u // D, tuple(range(CHUNKS)), lambda d, i: terms[u - 1 + d][:, at(i)], "out_bank")
+            if u % D == 0:
+                for c in range(ON_SCALAR, CHUNKS):
+                    scale_on_vector(terms[u][:, at(c)], odds[u][:, at(c)], 0, c)
+            else:
+                for c in range(CHUNKS):
+                    scale_and_add(terms[u][:, at(c)], odds[u][:, at(c)], 1, c, terms[u - 1][:, at(c)])
+                finish(u // D, tuple(range(CHUNKS)), lambda i: [terms[u][:, at(i)]], "out_bank")
 
         LAG = 4
         for u in range(whole):
@@ -163,16 +188,15 @@ def tile_picked_yndcg_lam_p_kernel(tc, x_words, x_scales, hT, delta, offs, pos1,
             if u >= LAG:
                 weigh_whole(u - LAG)
             if d == 0:
-                quantize(h_bf)
-                if b + 2 < BLOCKS:
-                    cast(b + 2, h_bf)
                 seed(u)
                 seed(u + 1)
-                product(b + 1, 0, S)
-            dst = fresh[u] if u < LAG else odds[u - LAG]
-            nc.vector.tensor_scalar(dst[:], scores[b][:].indirect(rivals[d][:]), -1.0, 0.0, MULT, ADD)
+            dst = fresh[u] if u < LAG else odds[u - LAG][:]
+            nc.vector.tensor_scalar(dst, scores[b][:].indirect(rivals[d][:]), -1.0, 0.0, MULT, ADD)
             turn(u, dst, 0, CHUNKS)
             squash(u)
+            if d == 0:
+                for c in range(ON_SCALAR):
+                    nc.scalar.activation(terms[u][:, at(c)], odds[u][:, at(c)], COPY, scale=factor(0, c))
 
         def small(u, d, dst):
             parts = units[u][1]
@@ -191,16 +215,19 @@ def tile_picked_yndcg_lam_p_kernel(tc, x_words, x_scales, hT, delta, offs, pos1,
         weigh_whole(4)
         seed(ub)
         small(ub, 0, odds[4][:, 0:P])
-        small(ub, 1, odds[4][:, P : 2 * P])
-        squash(ub)
         weigh_whole(5)
+        small(ub, 1, odds[5][:, 0:P])
+        squash(ub)
         seed(uc)
-        small(uc, 0, odds[5][:, 0:P])
-        small(uc, 1, odds[5][:, P : 2 * P])
+        small(uc, 0, odds[5][:, P : 2 * P])
+        small(uc, 1, odds[5][:, 2 * P : 3 * P])
         squash(uc)
-        weigh(ua)
-        finish(last, (0, 1), lambda d, i: terms[ua][:, at(2 * d + i)], "y_bank")
-        weigh(ub)
-        finish(last, (2,), lambda d, i: terms[ub][:, at(d)], "y_bank")
-        weigh(uc)
-        finish(last, (3,), lambda d, i: terms[uc][:, at(d)], "out_bank")
+        for c in (0, 1):
+            scale_on_vector(terms[ua][:, at(c)], odds[ua][:, at(c)], 0, c)
+        for c in (0, 1):
+            scale_and_add(terms[ua][:, at(2 + c)], odds[ua][:, at(2 + c)], 1, c, terms[ua][:, at(c)])
+        finish(last, (0, 1), lambda i: [terms[ua][:, at(2 + i)]], "y_bank")
+        for u, c, tag in ((ub, 2, "y_bank"), (uc, 3, "out_bank")):
+            for d in range(D):
+                scale_on_vector(terms[u][:, at(d)], odds[u][:, at(d)], d, c)
+            finish(last, (c,), lambda i: [terms[u][:, at(d)] for d in range(D)], tag)

@@ -4,12 +4,18 @@ import concourse.mybir as mybir
 from concourse.masks import make_identity
 
 K, T, S, V, D = 512, 1024, 512, 512, 2
+FLOPS = 2 * K * V * S
+
 P = 128
 PACK = 4
+PER_COLUMN = 16
 BLOCKS = V // P
 CHUNKS = S // P
-WINDOW = 2048
-FLOPS = 2 * K * V * S
+LAST = BLOCKS - 1
+HALF = S // 2
+WIDE = 2048
+LAG = 4
+ON_VECTOR = CHUNKS - 1
 
 F32 = mybir.dt.float32
 BF16 = mybir.dt.bfloat16
@@ -24,210 +30,221 @@ SIGMOID = mybir.ActivationFunctionType.Sigmoid
 COPY = mybir.ActivationFunctionType.Copy
 
 
+def span(first, count=1):
+    return slice(first * P, (first + count) * P)
+
+
+def entries(first, count):
+    return slice(first * P // PER_COLUMN, (first + count) * P // PER_COLUMN)
+
+
 def tile_picked_yndcg_lam_p_kernel(tc, x_words, x_scales, hT, delta, offs, pos1, pos2, out):
     nc = tc.nc
     with ExitStack() as ctx:
         keep = ctx.enter_context(tc.tile_pool(name="keep", bufs=1))
         psum = ctx.enter_context(tc.psum_pool(name="psum", bufs=1))
 
-        picks = keep.tile([P, S // 16], U16, name="picks")
-        rivals = [keep.tile([P, S // 16], U16, name="rivals%d" % d) for d in range(D)]
+        picks = keep.tile([P, S // PER_COLUMN], U16, name="picks")
+        rivals = [keep.tile([P, S // PER_COLUMN], U16, name="rivals%d" % d) for d in range(D)]
         words = keep.tile([P, T], U32, name="words", tag="words", align_bytes=64)
         scales = keep.tile([P, T], U8, name="scales", align_bytes=64)
-        h_first = keep.tile([P, P, PACK], BF16, name="h_first", tag="x_codes", align_bytes=64)
-        x_plane = keep.tile([P, S], U8, name="x_plane", align_bytes=64)
-        ident = keep.tile([P, P], F32, name="ident")
+        h_raw = [keep.tile([P, PACK, P], F32, name="h_raw%d" % b) for b in range(BLOCKS)]
+        h_rows = hT.rearrange("(p j) t -> p j t", j=PACK)
         warm = keep.tile([P, 8], F32, name="warm")
-        delta_rows = keep.tile([P, P], F32, name="delta_rows")
-        delta_cols = keep.tile([P, D * CHUNKS], F32, name="delta_cols")
 
         nc.vector.memset(scales[:].bitcast(I32), 0)
         nc.vector.memset(warm[:], 0.0)
-        h_rows = hT.rearrange("(p j) t -> p j t", j=PACK)
-        h_raw = [keep.tile([P, PACK, P], F32, name="h_raw%d" % b) for b in range(BLOCKS)]
-        nc.scalar.dma_start(h_raw[0][:], h_rows[:, :, 0:P])
+        nc.scalar.dma_start(h_raw[0][:], h_rows[:, :, span(0)])
         nc.sync.dma_start(picks[:], offs)
         for q in range(4):
-            (nc.sync, nc.scalar)[q % 2].dma_start(scales[32 * q : 32 * q + 4, :].bitcast(I32), x_scales[0, 4 * q : 4 * q + 4, :].bitcast(I32))
+            (nc.sync, nc.scalar)[q % 2].dma_start(
+                scales[32 * q : 32 * q + 4, :].bitcast(I32), x_scales[0, 4 * q : 4 * q + 4, :].bitcast(I32)
+            )
         nc.scalar.activation(warm[:, 0:1], warm[:, 1:2], SIGMOID)
         nc.sync.dma_start(words[:].bitcast(I32), x_words[0].rearrange("p n t -> p (n t)").bitcast(I32))
         for b in range(1, BLOCKS):
-            nc.sync.dma_start(h_raw[b][:], h_rows[:, :, b * P : (b + 1) * P])
+            nc.sync.dma_start(h_raw[b][:], h_rows[:, :, span(b)])
         nc.sync.dma_start(rivals[0][:], pos1)
         nc.sync.dma_start(rivals[1][:], pos2)
+
+        ident = keep.tile([P, P], F32, name="ident")
         make_identity(nc, ident[:])
+        delta_rows = keep.tile([P, P], F32, name="delta_rows")
+        delta_cols = keep.tile([P, D * CHUNKS], F32, name="delta_cols")
         nc.gpsimd.memset(delta_rows[:], 0.0)
         for d in range(D):
             nc.sync.dma_start(delta_rows[d * CHUNKS : (d + 1) * CHUNKS, :], delta[d, 0, :].rearrange("(c m) -> c m", m=P))
+        delta_end = keep.tile([P, D * P], F32, name="delta_end")
+        nc.sync.dma_start(
+            delta_end[:].rearrange("p (d m) -> p d m", d=D), delta[:, :, span(CHUNKS - 1)].rearrange("d p m -> p d m")
+        )
 
-        h_bf = [h_first] + [keep.tile([P, P, PACK], BF16, name="h_bf%d" % b, align_bytes=64) for b in (1, 2)]
-        h_codes = [keep.tile([P, P], U32, name="h_codes0", tag="relay", align_bytes=64)[:]]
-        h_plane = [keep.tile([P, P], U8, name="h_plane%d" % b, align_bytes=64) for b in range(BLOCKS)]
-        last = BLOCKS - 1
-        scores = [keep.tile([P, WINDOW], F32, name="scores%d" % b) for b in range(last)]
-        scores.append(keep.tile([P, S], F32, name="scores_last"))
+        h_first = keep.tile([P, P * PACK], BF16, name="h_first", tag="x_codes", align_bytes=64)
+        h_pair = keep.tile([P, 2 * P * PACK], BF16, name="h_pair", align_bytes=64)
+        codes_first = keep.tile([P, P], U32, name="codes_first", tag="relay", align_bytes=64)
+        codes_last = keep.tile([P, P], U32, name="codes_last", align_bytes=64)
+        bytes_first = keep.tile([P, P], U8, name="bytes_first", align_bytes=64)
+        bytes_pair = keep.tile([P, 2 * P], U8, name="bytes_pair", align_bytes=64)
+        bytes_last = keep.tile([P, P], U8, name="bytes_last", align_bytes=64)
+        x_bytes = keep.tile([P, S], U8, name="x_bytes", align_bytes=64)
+        scores = [keep.tile([P, S if b == LAST else WIDE], F32, name="scores%d" % b) for b in range(BLOCKS)]
         negated = keep.tile([P, S], F32, name="negated")
 
-        def cast(b):
+        def cast(b, dst):
             nc.scalar.copy(
-                h_bf[b][:].rearrange("p (c i) j -> p c j i", i=4),
+                dst.rearrange("p (c i j) -> p c j i", i=4, j=PACK),
                 h_raw[b][:].rearrange("p j (c i) -> p c j i", i=4),
             )
 
-        def quantize(b):
-            nc.vector.quantize_mx(out=h_codes[b].bitcast(FP8X4), scales=h_plane[b][:], in_=h_bf[b][:].rearrange("p t j -> p (t j)"))
+        def quantize(codes, scale_bytes, values):
+            nc.vector.quantize_mx(out=codes.bitcast(FP8X4), scales=scale_bytes, in_=values)
 
-        def product(b, lo, hi, tag):
-            bank = psum.tile([P, hi - lo], F32, name=tag, bufs=2)
+        def product(b, h_codes, h_bytes, cols, tag):
+            bank = psum.tile([P, cols.stop - cols.start], F32, name=tag, bufs=2)
             nc.tensor.matmul_mx(
                 out=bank[:],
-                lhsT=h_codes[b].bitcast(FP8X4),
-                lhsT_scale=h_plane[b][:],
-                rhs=x_codes[:, lo:hi].bitcast(FP8X4),
-                rhs_scale=x_plane[:, lo:hi],
+                lhsT=h_codes.bitcast(FP8X4),
+                lhsT_scale=h_bytes,
+                rhs=x_codes[:, cols].bitcast(FP8X4),
+                rhs_scale=x_bytes[:, cols],
                 start=True,
                 stop=True,
             )
-            if b == 0 and hi == S:
-                nc.vector.tensor_copy(scores[b][:, lo:hi], bank[:])
-            else:
-                nc.scalar.copy(scores[b][:, lo:hi], bank[:])
-            if b == last:
-                nc.scalar.activation(negated[:], bank[:], COPY, scale=-1.0)
+            nc.scalar.copy(scores[b][:, cols], bank[:])
+            return bank
 
-        half = S // 2
-        nc.vector.tensor_copy(x_plane[:], scales[:].indirect(picks[:]))
-        cast(0)
-        quantize(0)
-        cast(1)
-        cast(2)
+        nc.vector.tensor_copy(x_bytes[:], scales[:].indirect(picks[:]))
+        cast(0, h_first[:])
+        quantize(codes_first[:], bytes_first[:], h_first[:])
+        cast(1, h_pair[:, 0 : P * PACK])
+        cast(2, h_pair[:, P * PACK : 2 * P * PACK])
         x_codes = keep.tile([P, S], U32, name="x_codes", tag="x_codes", align_bytes=64)
-        for lo, hi, tag in ((0, half, "y_bank"), (half, half + P, "y_bank"), (half + P, S, "out_bank")):
-            nc.vector.tensor_copy(x_codes[:, lo:hi], words[:].indirect(picks[:, lo // 16 : hi // 16]))
-            product(0, lo, hi, tag)
-        h_later = keep.tile([P, last, P], U32, name="h_later", tag="words", align_bytes=64)
-        h_codes.extend(h_later[:, b, :] for b in range(last))
-        h_bf.append(keep.tile([P, P, PACK], BF16, name="h_bf3", tag="relay", align_bytes=64))
-        cast(3)
-        quantize(1)
-        product(1, 0, S, "out_bank")
-        quantize(2)
-        product(2, 0, S, "y_bank")
+        for first, count, tag in ((0, 2, "y_bank"), (2, 1, "y_bank"), (3, 1, "out_bank")):
+            nc.vector.tensor_copy(x_codes[:, span(first, count)], words[:].indirect(picks[:, entries(first, count)]))
+            product(0, codes_first[:], bytes_first[:], span(first, count), tag)
+
+        codes_pair = keep.tile([P, 2 * P], U32, name="codes_pair", tag="words", align_bytes=64)
+        h_last = keep.tile([P, P * PACK], BF16, name="h_last", tag="relay", align_bytes=64)
+        cast(LAST, h_last[:])
+        quantize(codes_pair[:], bytes_pair[:], h_pair[:])
+        product(1, codes_pair[:, span(0)], bytes_pair[:, span(0)], span(0, CHUNKS), "out_bank")
+        product(2, codes_pair[:, span(1)], bytes_pair[:, span(1)], span(0, CHUNKS), "y_bank")
 
         turned = psum.tile([P, P], F32, name="y_bank", bufs=2)
         nc.tensor.transpose(turned[:], delta_rows[:], ident[:])
         nc.scalar.copy(delta_cols[:], turned[:, 0 : D * CHUNKS])
 
-        quantize(3)
-        product(3, 0, S, "y_bank")
+        quantize(codes_last[:], bytes_last[:], h_last[:])
+        y_last = product(LAST, codes_last[:], bytes_last[:], span(0, CHUNKS), "y_bank")
+        nc.scalar.activation(negated[:], y_last[:], COPY, scale=-1.0)
 
-        units = [(b, [(d, c) for c in range(CHUNKS)]) for b in range(last) for d in range(D)]
-        whole = len(units)
-        for chunks in ((0, 1), (2,), (3,)):
-            units.append((last, [(d, c) for d in range(D) for c in chunks]))
-        odds = [keep.tile([P, len(un[1]) * P], F32, name="odds%d" % u) for u, un in enumerate(units)]
-        terms = [keep.tile([P, len(un[1]) * P], F32, name="terms%d" % u) for u, un in enumerate(units)]
-        first = keep.tile([P, S], F32, name="first")
-        early = keep.tile([P, 3 * S], F32, name="early", tag="relay", align_bytes=64)
-        fresh = [first[:]] + [early[:, n * S : (n + 1) * S] for n in range(3)]
-        diff = {}
+        def transpose_into(dst, src, start, stop):
+            nc.tensor.matmul(dst, src, ident[:], start=start, stop=stop, is_transpose=True)
 
-        def at(i):
-            return slice(i * P, (i + 1) * P)
+        def open_bank(own, chunks):
+            bank = psum.tile([P, len(chunks) * P], F32, name="diff_bank", bufs=4)
+            for i, c in enumerate(chunks):
+                transpose_into(bank[:, span(i)], own[:, span(c)], i == 0, False)
+            return bank
 
-        def seed(u):
-            b, parts = units[u]
-            bank = psum.tile([P, len(parts) * P], F32, name="diff_bank", bufs=4)
-            diff[u] = bank
-            own = negated if b == last else scores[b]
-            for i, (d, c) in enumerate(parts):
-                nc.tensor.matmul(bank[:, at(i)], own[:, at(c)], ident[:], start=(i == 0), stop=False, is_transpose=True)
-
-        def turn(u, src, first, count):
-            n = len(units[u][1])
+        def add_rivals(bank, fetched, first, count, closes):
             for i in range(count):
-                nc.tensor.matmul(diff[u][:, at(first + i)], src[:, at(i)], ident[:], start=False, stop=(first + i == n - 1), is_transpose=True)
+                transpose_into(bank[:, span(first + i)], fetched[:, span(i)], False, closes and i == count - 1)
 
-        def squash(u):
-            nc.scalar.activation(odds[u][:], diff[u][:], SIGMOID, scale=(1.0 if units[u][0] == last else -1.0))
+        def weight(d, c):
+            return delta_cols[:, d * CHUNKS + c : d * CHUNKS + c + 1]
 
-        def factor(d, c):
-            k = d * CHUNKS + c
-            return delta_cols[:, k : k + 1]
+        def weigh(dst, src, d, c):
+            nc.vector.tensor_scalar(dst, src, weight(d, c), None, MULT)
 
-        def scale_on_vector(dst, src, d, c):
-            nc.vector.tensor_scalar(dst, src, factor(d, c), None, MULT)
-
-        def scale_and_add(dst, src, d, c, other):
-            nc.vector.scalar_tensor_tensor(dst, src, factor(d, c), other, MULT, ADD)
-
-        def finish(b, chunks, sources, tag):
-            bank = psum.tile([P, len(chunks) * P], F32, name=tag, bufs=2)
-            for i in range(len(chunks)):
-                parts = sources(i)
+        def finish(b, first, count, addends, tag, queue):
+            bank = psum.tile([P, count * P], F32, name=tag, bufs=2)
+            for i in range(count):
+                parts = addends(i)
                 for n, part in enumerate(parts):
-                    nc.tensor.matmul(bank[:, at(i)], part, ident[:], start=(n == 0), stop=(n == len(parts) - 1), is_transpose=True)
-            result = keep.tile([P, len(chunks) * P], F32, name="result%d_%d" % (b, chunks[0]))
+                    transpose_into(bank[:, span(i)], part, n == 0, n == len(parts) - 1)
+            result = keep.tile([P, count * P], F32, name="result%d_%d" % (b, first))
             nc.scalar.copy(result[:], bank[:])
-            nc.sync.dma_start(out[at(b), chunks[0] * P : (chunks[-1] + 1) * P], result[:])
+            queue.dma_start(out[span(b), span(first, count)], result[:])
 
-        ON_SCALAR = 2
+        units = LAST * D
+        lead = S - P
+        room = [keep.tile([P, lead + S], F32, name="room%d" % u) for u in range(units)]
+        odds = [room[u][:, lead : lead + S] for u in range(units)]
+        terms = [keep.tile([P, S], F32, name="terms%d" % u) for u in range(units)]
+        opening = keep.tile([P, S], F32, name="opening")
+        early = keep.tile([P, (LAG - 1) * S], F32, name="early", tag="relay", align_bytes=64)
+        fresh = [opening[:]] + [early[:, n * S : (n + 1) * S] for n in range(LAG - 1)]
+        summed_on_vector = LAST - 1
 
-        def weigh_whole(u):
-            if u % D == 0:
-                for c in range(ON_SCALAR, CHUNKS):
-                    scale_on_vector(terms[u][:, at(c)], odds[u][:, at(c)], 0, c)
-            else:
+        def weigh_unit(u):
+            b, d = divmod(u, D)
+            if b == summed_on_vector and d == D - 1:
                 for c in range(CHUNKS):
-                    scale_and_add(terms[u][:, at(c)], odds[u][:, at(c)], 1, c, terms[u - 1][:, at(c)])
-                finish(u // D, tuple(range(CHUNKS)), lambda i: [terms[u][:, at(i)]], "out_bank")
+                    nc.vector.scalar_tensor_tensor(
+                        terms[u][:, span(c)], odds[u][:, span(c)], weight(d, c), terms[u - 1][:, span(c)], MULT, ADD
+                    )
+                finish(b, 0, CHUNKS, lambda i: [terms[u][:, span(i)]], "out_bank", nc.sync)
+                return
+            for c in range(CHUNKS if b == summed_on_vector else ON_VECTOR):
+                weigh(terms[u][:, span(c)], odds[u][:, span(c)], d, c)
+            if d == D - 1:
+                finish(b, 0, CHUNKS, lambda i: [terms[u - 1][:, span(i)], terms[u][:, span(i)]], "out_bank", nc.sync)
 
-        LAG = 4
-        for u in range(whole):
-            b, d = u // D, u % D
+        banks = []
+        for u in range(units):
+            b, d = divmod(u, D)
             if u >= LAG:
-                weigh_whole(u - LAG)
+                weigh_unit(u - LAG)
             if d == 0:
-                seed(u)
-                seed(u + 1)
-            dst = fresh[u] if u < LAG else odds[u - LAG][:]
-            nc.vector.tensor_scalar(dst, scores[b][:].indirect(rivals[d][:]), -1.0, 0.0, MULT, ADD)
-            turn(u, dst, 0, CHUNKS)
-            squash(u)
-            if d == 0:
-                for c in range(ON_SCALAR):
-                    nc.scalar.activation(terms[u][:, at(c)], odds[u][:, at(c)], COPY, scale=factor(0, c))
+                banks.extend([open_bank(scores[b], range(CHUNKS)) for n in range(D)])
+            fetched = fresh[u] if u < LAG else room[u - LAG][:, 0:S]
+            nc.vector.tensor_scalar(fetched, scores[b][:].indirect(rivals[d][:]), -1.0, 0.0, MULT, ADD)
+            add_rivals(banks[u], fetched, 0, CHUNKS, True)
+            nc.scalar.activation(odds[u], banks[u][:], SIGMOID, scale=-1.0)
+            if b != summed_on_vector:
+                for c in range(ON_VECTOR, CHUNKS):
+                    nc.scalar.activation(terms[u][:, span(c)], odds[u][:, span(c)], COPY, scale=weight(d, c))
 
-        def small(u, d, dst):
-            parts = units[u][1]
-            n = len(parts) // D
-            c0 = parts[0][1]
-            nc.vector.tensor_copy(dst, scores[last][:].indirect(rivals[d][:, c0 * 8 : (c0 + n) * 8]))
-            turn(u, dst, d * n, n)
+        def fetch(bank, d, first, count, fetched):
+            nc.vector.tensor_copy(fetched, scores[LAST][:].indirect(rivals[d][:, entries(first, count)]))
+            add_rivals(bank, fetched, d * count, count, d == D - 1)
 
-        ua, ub, uc = whole, whole + 1, whole + 2
-        weigh_whole(2)
-        seed(ua)
-        small(ua, 0, odds[2][:, 0:half])
-        weigh_whole(3)
-        small(ua, 1, odds[3][:, 0:half])
-        squash(ua)
-        weigh_whole(4)
-        seed(ub)
-        small(ub, 0, odds[4][:, 0:P])
-        weigh_whole(5)
-        small(ub, 1, odds[5][:, 0:P])
-        squash(ub)
-        seed(uc)
-        small(uc, 0, odds[5][:, P : 2 * P])
-        small(uc, 1, odds[5][:, 2 * P : 3 * P])
-        squash(uc)
-        for c in (0, 1):
-            scale_on_vector(terms[ua][:, at(c)], odds[ua][:, at(c)], 0, c)
-        for c in (0, 1):
-            scale_and_add(terms[ua][:, at(2 + c)], odds[ua][:, at(2 + c)], 1, c, terms[ua][:, at(c)])
-        finish(last, (0, 1), lambda i: [terms[ua][:, at(2 + i)]], "y_bank")
-        for u, c, tag in ((ub, 2, "y_bank"), (uc, 3, "out_bank")):
+        def weigh_piece(piece_odds, first, count, queue):
+            piece_terms = keep.tile([P, D * count * P], F32, name="piece_terms%d" % first)
             for d in range(D):
-                scale_on_vector(terms[u][:, at(d)], odds[u][:, at(d)], d, c)
-            finish(last, (c,), lambda i: [terms[u][:, at(d)] for d in range(D)], tag)
+                for i in range(count):
+                    weigh(piece_terms[:, span(d * count + i)], piece_odds[:, span(d * count + i)], d, first + i)
+            finish(LAST, first, count, lambda i: [piece_terms[:, span(d * count + i)] for d in range(D)], "y_bank", queue)
+
+        pending = units - LAG
+        odds_front = keep.tile([P, D * 2 * P], F32, name="odds_front")
+        odds_middle = keep.tile([P, D * P], F32, name="odds_middle")
+        odds_end = keep.tile([P, D * P], F32, name="odds_end")
+
+        weigh_unit(pending)
+        front = open_bank(negated, (0, 1) * D)
+        fetch(front, 0, 0, 2, room[pending][:, HALF:S])
+        weigh_unit(pending + 1)
+        fetch(front, 1, 0, 2, room[pending + 1][:, HALF:S])
+        nc.scalar.activation(odds_front[:], front[:], SIGMOID)
+
+        weigh_unit(pending + 2)
+        middle = open_bank(negated, (2,) * D)
+        for d in range(D):
+            fetch(middle, d, 2, 1, odds[pending + 2][:, span(d)])
+        nc.scalar.activation(odds_middle[:], middle[:], SIGMOID)
+
+        weigh_unit(pending + 3)
+        gaps = odds[pending + 3][:, span(0, D)]
+        for d in range(D):
+            nc.vector.tensor_tensor(gaps[:, span(d)], scores[LAST][:].indirect(rivals[d][:, entries(3, 1)]), negated[:, span(3)], ADD)
+        nc.scalar.activation(odds_end[:], gaps, SIGMOID)
+
+        weigh_piece(odds_front, 0, 2, nc.sync)
+        weigh_piece(odds_middle, 2, 1, nc.scalar)
+        terms_end = keep.tile([P, D * P], F32, name="terms_end")
+        result_end = keep.tile([P, P], F32, name="result_end")
+        nc.vector.tensor_tensor(terms_end[:], odds_end[:], delta_end[:], MULT)
+        nc.vector.tensor_tensor(result_end[:], terms_end[:, span(0)], terms_end[:, span(1)], ADD)
+        nc.sync.dma_start(out[span(LAST), span(3)], result_end[:])

@@ -80,12 +80,12 @@ def tile_picked_yndcg_lam_p_kernel(tc, x_words, x_scales, hT, delta, offs, pos1,
         )
 
         h_first = keep.tile([P, P * PACK], BF16, name="h_first", tag="x_codes", align_bytes=64)
-        h_pair = keep.tile([P, 2 * P * PACK], BF16, name="h_pair", align_bytes=64)
+        h_second = keep.tile([P, P * PACK], BF16, name="h_second", align_bytes=64)
         codes_first = keep.tile([P, P], U32, name="codes_first", tag="relay", align_bytes=64)
-        codes_last = keep.tile([P, P], U32, name="codes_last", align_bytes=64)
+        codes_pair = keep.tile([P, 2 * P], U32, name="codes_pair", align_bytes=64)
         bytes_first = keep.tile([P, P], U8, name="bytes_first", align_bytes=64)
+        bytes_second = keep.tile([P, P], U8, name="bytes_second", align_bytes=64)
         bytes_pair = keep.tile([P, 2 * P], U8, name="bytes_pair", align_bytes=64)
-        bytes_last = keep.tile([P, P], U8, name="bytes_last", align_bytes=64)
         x_bytes = keep.tile([P, S], U8, name="x_bytes", align_bytes=64)
         scores = [keep.tile([P, S if b == LAST else WIDE], F32, name="scores%d" % b) for b in range(BLOCKS)]
         negated = keep.tile([P, S], F32, name="negated")
@@ -116,27 +116,24 @@ def tile_picked_yndcg_lam_p_kernel(tc, x_words, x_scales, hT, delta, offs, pos1,
         nc.vector.tensor_copy(x_bytes[:], scales[:].indirect(picks[:]))
         cast(0, h_first[:])
         quantize(codes_first[:], bytes_first[:], h_first[:])
-        cast(1, h_pair[:, 0 : P * PACK])
-        cast(2, h_pair[:, P * PACK : 2 * P * PACK])
+        cast(1, h_second[:])
         x_codes = keep.tile([P, S], U32, name="x_codes", tag="x_codes", align_bytes=64)
         for first, count, tag in ((0, 2, "y_bank"), (2, 1, "y_bank"), (3, 1, "out_bank")):
             nc.vector.tensor_copy(x_codes[:, span(first, count)], words[:].indirect(picks[:, entries(first, count)]))
             product(0, codes_first[:], bytes_first[:], span(first, count), tag)
 
-        codes_pair = keep.tile([P, 2 * P], U32, name="codes_pair", tag="words", align_bytes=64)
-        h_last = keep.tile([P, P * PACK], BF16, name="h_last", tag="relay", align_bytes=64)
-        cast(LAST, h_last[:])
-        quantize(codes_pair[:], bytes_pair[:], h_pair[:])
-        product(1, codes_pair[:, span(0)], bytes_pair[:, span(0)], span(0, CHUNKS), "out_bank")
-        product(2, codes_pair[:, span(1)], bytes_pair[:, span(1)], span(0, CHUNKS), "y_bank")
+        codes_second = keep.tile([P, P], U32, name="codes_second", tag="words", align_bytes=64)
+        h_pair = keep.tile([P, 2 * P * PACK], BF16, name="h_pair", tag="relay", align_bytes=64)
+        cast(2, h_pair[:, 0 : P * PACK])
+        cast(3, h_pair[:, P * PACK : 2 * P * PACK])
+        quantize(codes_second[:], bytes_second[:], h_second[:])
+        product(1, codes_second[:], bytes_second[:], span(0, CHUNKS), "out_bank")
 
         turned = psum.tile([P, P], F32, name="y_bank", bufs=2)
         nc.tensor.transpose(turned[:], delta_rows[:], ident[:])
         nc.scalar.copy(delta_cols[:], turned[:, 0 : D * CHUNKS])
 
-        quantize(codes_last[:], bytes_last[:], h_last[:])
-        y_last = product(LAST, codes_last[:], bytes_last[:], span(0, CHUNKS), "y_bank")
-        nc.scalar.activation(negated[:], y_last[:], COPY, scale=-1.0)
+        quantize(codes_pair[:], bytes_pair[:], h_pair[:])
 
         def transpose_into(dst, src, start, stop):
             nc.tensor.matmul(dst, src, ident[:], start=start, stop=stop, is_transpose=True)
@@ -175,18 +172,20 @@ def tile_picked_yndcg_lam_p_kernel(tc, x_words, x_scales, hT, delta, offs, pos1,
         opening = keep.tile([P, S], F32, name="opening")
         early = keep.tile([P, (LAG - 1) * S], F32, name="early", tag="relay", align_bytes=64)
         fresh = [opening[:]] + [early[:, n * S : (n + 1) * S] for n in range(LAG - 1)]
-        summed_on_vector = LAST - 1
+
+        def adds_on_vector(b, d):
+            return b == LAST - 1 and d == D - 1
 
         def weigh_unit(u):
             b, d = divmod(u, D)
-            if b == summed_on_vector and d == D - 1:
+            if adds_on_vector(b, d):
                 for c in range(CHUNKS):
                     nc.vector.scalar_tensor_tensor(
                         terms[u][:, span(c)], odds[u][:, span(c)], weight(d, c), terms[u - 1][:, span(c)], MULT, ADD
                     )
                 finish(b, 0, CHUNKS, lambda i: [terms[u][:, span(i)]], "out_bank", nc.sync)
                 return
-            for c in range(CHUNKS if b == summed_on_vector else ON_VECTOR):
+            for c in range(ON_VECTOR):
                 weigh(terms[u][:, span(c)], odds[u][:, span(c)], d, c)
             if d == D - 1:
                 finish(b, 0, CHUNKS, lambda i: [terms[u - 1][:, span(i)], terms[u][:, span(i)]], "out_bank", nc.sync)
@@ -202,9 +201,13 @@ def tile_picked_yndcg_lam_p_kernel(tc, x_words, x_scales, hT, delta, offs, pos1,
             nc.vector.tensor_scalar(fetched, scores[b][:].indirect(rivals[d][:]), -1.0, 0.0, MULT, ADD)
             add_rivals(banks[u], fetched, 0, CHUNKS, True)
             nc.scalar.activation(odds[u], banks[u][:], SIGMOID, scale=-1.0)
-            if b != summed_on_vector:
+            if not adds_on_vector(b, d):
                 for c in range(ON_VECTOR, CHUNKS):
                     nc.scalar.activation(terms[u][:, span(c)], odds[u][:, span(c)], COPY, scale=weight(d, c))
+            if u == 0:
+                product(2, codes_pair[:, span(0)], bytes_pair[:, span(0)], span(0, CHUNKS), "y_bank")
+                y_last = product(LAST, codes_pair[:, span(1)], bytes_pair[:, span(1)], span(0, CHUNKS), "y_bank")
+                nc.scalar.activation(negated[:], y_last[:], COPY, scale=-1.0)
 
         def fetch(bank, d, first, count, fetched):
             nc.vector.tensor_copy(fetched, scores[LAST][:].indirect(rivals[d][:, entries(first, count)]))
@@ -220,7 +223,6 @@ def tile_picked_yndcg_lam_p_kernel(tc, x_words, x_scales, hT, delta, offs, pos1,
         pending = units - LAG
         odds_front = keep.tile([P, D * 2 * P], F32, name="odds_front")
         odds_middle = keep.tile([P, D * P], F32, name="odds_middle")
-        odds_end = keep.tile([P, D * P], F32, name="odds_end")
 
         weigh_unit(pending)
         front = open_bank(negated, (0, 1) * D)
@@ -239,12 +241,13 @@ def tile_picked_yndcg_lam_p_kernel(tc, x_words, x_scales, hT, delta, offs, pos1,
         gaps = odds[pending + 3][:, span(0, D)]
         for d in range(D):
             nc.vector.tensor_tensor(gaps[:, span(d)], scores[LAST][:].indirect(rivals[d][:, entries(3, 1)]), negated[:, span(3)], ADD)
-        nc.scalar.activation(odds_end[:], gaps, SIGMOID)
 
         weigh_piece(odds_front, 0, 2, nc.sync)
+        odds_end = odds_front[:, span(0, D)]
+        nc.scalar.activation(odds_end, gaps, SIGMOID)
         weigh_piece(odds_middle, 2, 1, nc.scalar)
         terms_end = keep.tile([P, D * P], F32, name="terms_end")
         result_end = keep.tile([P, P], F32, name="result_end")
-        nc.vector.tensor_tensor(terms_end[:], odds_end[:], delta_end[:], MULT)
+        nc.vector.tensor_tensor(terms_end[:], odds_end, delta_end[:], MULT)
         nc.vector.tensor_tensor(result_end[:], terms_end[:, span(0)], terms_end[:, span(1)], ADD)
         nc.sync.dma_start(out[span(LAST), span(3)], result_end[:])

from contextlib import ExitStack

import concourse.mybir as mybir
from concourse.masks import make_identity

K, T, S, V, D = 512, 1024, 512, 512, 2
FLOPS = 2 * K * V * S

P = 128
PACK = 4
PER_COLUMN = 16
BLOCKS = V // P
CHUNKS = S // P
LAST = BLOCKS - 1
HALF = S // 2
WIDE = 2048
LAG = 4
ON_VECTOR = CHUNKS - 1

F32 = mybir.dt.float32
BF16 = mybir.dt.bfloat16
I32 = mybir.dt.int32
U32 = mybir.dt.uint32
U16 = mybir.dt.uint16
U8 = mybir.dt.uint8
FP8X4 = mybir.dt.float8_e4m3fn_x4
MULT = mybir.AluOpType.mult
ADD = mybir.AluOpType.add
SIGMOID = mybir.ActivationFunctionType.Sigmoid
COPY = mybir.ActivationFunctionType.Copy


def span(first, count=1):
    return slice(first * P, (first + count) * P)


def entries(first, count):
    return slice(first * P // PER_COLUMN, (first + count) * P // PER_COLUMN)


def tile_picked_yndcg_lam_p_kernel(tc, x_words, x_scales, hT, delta, offs, pos1, pos2, out):
    nc = tc.nc
    with ExitStack() as ctx:
        keep = ctx.enter_context(tc.tile_pool(name="keep", bufs=1))
        psum = ctx.enter_context(tc.psum_pool(name="psum", bufs=1))

        picks = keep.tile([P, S // PER_COLUMN], U16, name="picks")
        rivals = [keep.tile([P, S // PER_COLUMN], U16, name="rivals%d" % d) for d in range(D)]
        words = keep.tile([P, T], U32, name="words", tag="words", align_bytes=64)
        scales = keep.tile([P, T], U8, name="scales", align_bytes=64)
        h_raw = [keep.tile([P, PACK, P], F32, name="h_raw%d" % b) for b in range(BLOCKS)]
        h_rows = hT.rearrange("(p j) t -> p j t", j=PACK)
        warm = keep.tile([P, 8], F32, name="warm")

        nc.vector.memset(scales[:].bitcast(I32), 0)
        nc.vector.memset(warm[:], 0.0)
        nc.scalar.dma_start(h_raw[0][:], h_rows[:, :, span(0)])
        nc.sync.dma_start(picks[:], offs)
        for q in range(4):
            (nc.sync, nc.scalar)[q % 2].dma_start(
                scales[32 * q : 32 * q + 4, :].bitcast(I32), x_scales[0, 4 * q : 4 * q + 4, :].bitcast(I32)
            )
        nc.scalar.activation(warm[:, 0:1], warm[:, 1:2], SIGMOID)
        nc.sync.dma_start(words[:].bitcast(I32), x_words[0].rearrange("p n t -> p (n t)").bitcast(I32))
        for b in range(1, BLOCKS):
            nc.sync.dma_start(h_raw[b][:], h_rows[:, :, span(b)])
        nc.sync.dma_start(rivals[0][:], pos1)
        nc.sync.dma_start(rivals[1][:], pos2)

        ident = keep.tile([P, P], F32, name="ident")
        make_identity(nc, ident[:])
        delta_rows = keep.tile([P, P], F32, name="delta_rows")
        delta_cols = keep.tile([P, D * CHUNKS], F32, name="delta_cols")
        nc.gpsimd.memset(delta_rows[:], 0.0)
        for d in range(D):
            nc.sync.dma_start(delta_rows[d * CHUNKS : (d + 1) * CHUNKS, :], delta[d, 0, :].rearrange("(c m) -> c m", m=P))
        delta_end = keep.tile([P, D * P], F32, name="delta_end")
        nc.sync.dma_start(
            delta_end[:].rearrange("p (d m) -> p d m", d=D), delta[:, :, span(CHUNKS - 1)].rearrange("d p m -> p d m")
        )

        h_first = keep.tile([P, P * PACK], BF16, name="h_first", tag="x_codes", align_bytes=64)
        h_second = keep.tile([P, P * PACK], BF16, name="h_second", align_bytes=64)
        codes_first = keep.tile([P, P], U32, name="codes_first", tag="relay", align_bytes=64)
        codes_pair = keep.tile([P, 2 * P], U32, name="codes_pair", align_bytes=64)
        bytes_first = keep.tile([P, P], U8, name="bytes_first", align_bytes=64)
        bytes_second = keep.tile([P, P], U8, name="bytes_second", align_bytes=64)
        bytes_pair = keep.tile([P, 2 * P], U8, name="bytes_pair", align_bytes=64)
        x_bytes = keep.tile([P, S], U8, name="x_bytes", align_bytes=64)
        scores = [keep.tile([P, S if b == LAST else WIDE], F32, name="scores%d" % b) for b in range(BLOCKS)]
        negated = keep.tile([P, S], F32, name="negated")

        def cast(b, dst):
            nc.scalar.copy(
                dst.rearrange("p (c i j) -> p c j i", i=4, j=PACK),
                h_raw[b][:].rearrange("p j (c i) -> p c j i", i=4),
            )

        def quantize(codes, scale_bytes, values):
            nc.vector.quantize_mx(out=codes.bitcast(FP8X4), scales=scale_bytes, in_=values)

        def product(b, h_codes, h_bytes, cols, tag):
            bank = psum.tile([P, cols.stop - cols.start], F32, name=tag, bufs=2)
            nc.tensor.matmul_mx(
                out=bank[:],
                lhsT=h_codes.bitcast(FP8X4),
                lhsT_scale=h_bytes,
                rhs=x_codes[:, cols].bitcast(FP8X4),
                rhs_scale=x_bytes[:, cols],
                start=True,
                stop=True,
            )
            nc.scalar.copy(scores[b][:, cols], bank[:])
            return bank

        nc.vector.tensor_copy(x_bytes[:], scales[:].indirect(picks[:]))
        cast(0, h_first[:])
        quantize(codes_first[:], bytes_first[:], h_first[:])
        cast(1, h_second[:])
        x_codes = keep.tile([P, S], U32, name="x_codes", tag="x_codes", align_bytes=64)
        for first, count, tag in ((0, 2, "y_bank"), (2, 1, "y_bank"), (3, 1, "out_bank")):
            nc.vector.tensor_copy(x_codes[:, span(first, count)], words[:].indirect(picks[:, entries(first, count)]))
            product(0, codes_first[:], bytes_first[:], span(first, count), tag)

        codes_second = keep.tile([P, P], U32, name="codes_second", tag="words", align_bytes=64)
        h_pair = keep.tile([P, 2 * P * PACK], BF16, name="h_pair", tag="relay", align_bytes=64)
        cast(2, h_pair[:, 0 : P * PACK])
        cast(3, h_pair[:, P * PACK : 2 * P * PACK])
        quantize(codes_second[:], bytes_second[:], h_second[:])
        product(1, codes_second[:], bytes_second[:], span(0, CHUNKS), "out_bank")

        turned = psum.tile([P, P], F32, name="y_bank", bufs=2)
        nc.tensor.transpose(turned[:], delta_rows[:], ident[:])
        nc.scalar.copy(delta_cols[:], turned[:, 0 : D * CHUNKS])

        quantize(codes_pair[:], bytes_pair[:], h_pair[:])

        def transpose_into(dst, src, start, stop):
            nc.tensor.matmul(dst, src, ident[:], start=start, stop=stop, is_transpose=True)

        def open_bank(own, chunks):
            bank = psum.tile([P, len(chunks) * P], F32, name="diff_bank", bufs=4)
            for i, c in enumerate(chunks):
                transpose_into(bank[:, span(i)], own[:, span(c)], i == 0, False)
            return bank

        def add_rivals(bank, fetched, first, count, closes):
            for i in range(count):
                transpose_into(bank[:, span(first + i)], fetched[:, span(i)], False, closes and i == count - 1)

        def weight(d, c):
            return delta_cols[:, d * CHUNKS + c : d * CHUNKS + c + 1]

        def weigh(dst, src, d, c):
            nc.vector.tensor_scalar(dst, src, weight(d, c), None, MULT)

        def finish(b, first, count, addends, tag, queue):
            bank = psum.tile([P, count * P], F32, name=tag, bufs=2)
            for i in range(count):
                parts = addends(i)
                for n, part in enumerate(parts):
                    transpose_into(bank[:, span(i)], part, n == 0, n == len(parts) - 1)
            result = keep.tile([P, count * P], F32, name="result%d_%d" % (b, first))
            nc.scalar.copy(result[:], bank[:])
            queue.dma_start(out[span(b), span(first, count)], result[:])

        units = LAST * D
        lead = S - P
        room = [keep.tile([P, lead + S], F32, name="room%d" % u) for u in range(units)]
        odds = [room[u][:, lead : lead + S] for u in range(units)]
        terms = [keep.tile([P, S], F32, name="terms%d" % u) for u in range(units)]
        opening = keep.tile([P, S], F32, name="opening")
        early = keep.tile([P, (LAG - 1) * S], F32, name="early", tag="relay", align_bytes=64)
        fresh = [opening[:]] + [early[:, n * S : (n + 1) * S] for n in range(LAG - 1)]

        def adds_on_vector(b, d):
            return b == LAST - 1 and d == D - 1

        def weigh_unit(u):
            b, d = divmod(u, D)
            if adds_on_vector(b, d):
                for c in range(CHUNKS):
                    nc.vector.scalar_tensor_tensor(
                        terms[u][:, span(c)], odds[u][:, span(c)], weight(d, c), terms[u - 1][:, span(c)], MULT, ADD
                    )
                finish(b, 0, CHUNKS, lambda i: [terms[u][:, span(i)]], "out_bank", nc.sync)
                return
            for c in range(ON_VECTOR):
                weigh(terms[u][:, span(c)], odds[u][:, span(c)], d, c)
            if d == D - 1:
                finish(b, 0, CHUNKS, lambda i: [terms[u - 1][:, span(i)], terms[u][:, span(i)]], "out_bank", nc.sync)

        banks = []
        for u in range(units):
            b, d = divmod(u, D)
            if u >= LAG:
                weigh_unit(u - LAG)
            if d == 0:
                banks.extend([open_bank(scores[b], range(CHUNKS)) for n in range(D)])
            fetched = fresh[u] if u < LAG else room[u - LAG][:, 0:S]
            nc.vector.tensor_scalar(fetched, scores[b][:].indirect(rivals[d][:]), -1.0, 0.0, MULT, ADD)
            add_rivals(banks[u], fetched, 0, CHUNKS, True)
            nc.scalar.activation(odds[u], banks[u][:], SIGMOID, scale=-1.0)
            if not adds_on_vector(b, d):
                for c in range(ON_VECTOR, CHUNKS):
                    nc.scalar.activation(terms[u][:, span(c)], odds[u][:, span(c)], COPY, scale=weight(d, c))
            if u == 0:
                product(2, codes_pair[:, span(0)], bytes_pair[:, span(0)], span(0, CHUNKS), "y_bank")
                y_last = product(LAST, codes_pair[:, span(1)], bytes_pair[:, span(1)], span(0, CHUNKS), "y_bank")
                nc.scalar.activation(negated[:], y_last[:], COPY, scale=-1.0)

        def fetch(bank, d, first, count, fetched):
            nc.vector.tensor_copy(fetched, scores[LAST][:].indirect(rivals[d][:, entries(first, count)]))
            add_rivals(bank, fetched, d * count, count, d == D - 1)

        def weigh_piece(piece_odds, first, count, queue):
            piece_terms = keep.tile([P, D * count * P], F32, name="piece_terms%d" % first)
            for d in range(D):
                for i in range(count):
                    weigh(piece_terms[:, span(d * count + i)], piece_odds[:, span(d * count + i)], d, first + i)
            finish(LAST, first, count, lambda i: [piece_terms[:, span(d * count + i)] for d in range(D)], "y_bank", queue)

        pending = units - LAG
        odds_front = keep.tile([P, D * 2 * P], F32, name="odds_front")
        odds_middle = keep.tile([P, D * P], F32, name="odds_middle")

        weigh_unit(pending)
        front = open_bank(negated, (0, 1) * D)
        fetch(front, 0, 0, 2, room[pending][:, HALF:S])
        weigh_unit(pending + 1)
        fetch(front, 1, 0, 2, room[pending + 1][:, HALF:S])
        nc.scalar.activation(odds_front[:], front[:], SIGMOID)

        weigh_unit(pending + 2)
        middle = open_bank(negated, (2,) * D)
        for d in range(D):
            fetch(middle, d, 2, 1, odds[pending + 2][:, span(d)])
        nc.scalar.activation(odds_middle[:], middle[:], SIGMOID)

        weigh_unit(pending + 3)
        gaps = odds[pending + 3][:, span(0, D)]
        for d in range(D):
            nc.vector.tensor_tensor(gaps[:, span(d)], scores[LAST][:].indirect(rivals[d][:, entries(3, 1)]), negated[:, span(3)], ADD)

        weigh_piece(odds_front, 0, 2, nc.sync)
        odds_end = odds_front[:, span(0, D)]
        nc.scalar.activation(odds_end, gaps, SIGMOID)
        weigh_piece(odds_middle, 2, 1, nc.scalar)
        terms_end = keep.tile([P, D * P], F32, name="terms_end")
        result_end = keep.tile([P, P], F32, name="result_end")
        nc.vector.tensor_tensor(terms_end[:], odds_end, delta_end[:], MULT)
        nc.vector.tensor_tensor(result_end[:], terms_end[:, span(0)], terms_end[:, span(1)], ADD)
        nc.sync.dma_start(out[span(LAST), span(3)], result_end[:])
